import numpy as np
import ml_dtypes


def mxq(x, axis, fmt="e4m3"):
    dtype, down = {"e4m3": (ml_dtypes.float8_e4m3fn, 7), "e5m2": (ml_dtypes.float8_e5m2, 14)}[fmt]
    v = np.moveaxis(np.asarray(x, np.float32).astype(ml_dtypes.bfloat16).astype(np.float64), axis, -1)
    blocks = v.reshape(v.shape[:-1] + (-1, 32))
    amax = np.abs(blocks).max(-1, keepdims=True)
    byte = np.maximum(np.where(amax > 0, np.frexp(amax)[1] - 1 + 127, 0) - down, 1)
    scale = np.exp2(byte - 127.0)
    codes = (blocks / scale).astype(np.float32).astype(dtype).astype(np.float64)
    return np.moveaxis((codes * scale).reshape(v.shape), -1, axis)


WIDE = False


def mx_kscale(k):
    if not WIDE:
        return np.ones(k)
    levels = np.array([30, -30])
    if k % 512:
        return np.exp2(np.random.permutation(np.resize(levels, k // 32))).repeat(32)
    a = np.empty((k // 512, 16))
    for p in range(k // 512):
        a[p, :8] = np.random.permutation(np.resize(levels, 8))
        for g in range(8):
            far = levels[np.abs(levels - a[p, g]) >= 10]
            a[p, g + 8] = far[np.random.randint(len(far))]
    return np.exp2(a.ravel()).repeat(32)


def f64(x):
    return np.asarray(x).astype(np.float64)


def striped(idx):
    return np.tile(np.asarray(idx).reshape(-1, 16).T, (8, 1)).astype(np.uint16)


def unstriped(offs):
    return offs[:16].T.reshape(-1).astype(np.int64)


def striped8(idx):
    return np.asarray(idx).reshape(8, -1, 16).transpose(0, 2, 1).reshape(128, -1).astype(np.uint16)


def unstriped8(offs):
    return offs.reshape(8, 16, -1).transpose(0, 2, 1).reshape(8, -1).astype(np.int64)


def pick8(x, idx, run):
    r = np.arange(len(x))
    return x[r[:, None], idx[r % (8 * run) // run]]


E2M1 = np.array([0.0, 0.5, 1.0, 1.5, 2.0, 3.0, 4.0, 6.0, -0.0, -0.5, -1.0, -1.5, -2.0, -3.0, -4.0, -6.0])


def pack_weight(w, fmt):
    k, n = w.shape
    w = f64(np.asarray(w, np.float32).astype(ml_dtypes.bfloat16)).reshape(k // 32, 32, n)
    amax = np.abs(w).max(1)
    if fmt in ("e4m3", "e5m2"):
        byte = np.frexp(amax)[1] - 1 + 127 - (7 if fmt == "e4m3" else 14)
    else:
        mant, ex = np.frexp(amax / 6.0)
        byte = np.where(mant > 0.5, ex, ex - 1) + 127
    byte = np.clip(np.where(amax > 0, byte, 1), 1, 254)
    scaled = (w * np.exp2(127.0 - byte)[:, None, :]).reshape(k, n).astype(np.float32)
    by_word = np.ascontiguousarray(scaled.reshape(k // 512, 128, 4, n).transpose(0, 1, 3, 2))
    if fmt in ("e4m3", "e5m2"):
        words = by_word.astype(ml_dtypes.float8_e4m3fn if fmt == "e4m3" else ml_dtypes.float8_e5m2).view(np.uint8)
    else:
        c = by_word.astype(ml_dtypes.float4_e2m1fn).view(np.uint8) & 0xF
        words = (c[..., 0::2] | (c[..., 1::2] << 4)).reshape(k // 512, 128, 2 * n)
    return np.ascontiguousarray(words), np.ascontiguousarray(byte.astype(np.uint8).reshape(k // 512, 16, n))


def unpack_weight(words, scales, fmt):
    g, _, n = scales.shape
    words = np.ascontiguousarray(words).reshape(g, 128, n, -1)
    if fmt in ("e4m3", "e5m2"):
        vals = words.view(ml_dtypes.float8_e4m3fn if fmt == "e4m3" else ml_dtypes.float8_e5m2).astype(np.float64)
    else:
        nib = np.empty((g, 128, n, 4), np.uint8)
        nib[..., 0::2] = words & 0xF
        nib[..., 1::2] = words >> 4
        vals = E2M1[nib]
    vals = vals * np.repeat(np.exp2(scales.astype(np.float64) - 127.0), 8, axis=1)[..., None]
    return vals.transpose(0, 1, 3, 2).reshape(g * 512, n)


K, T, J, R, C, I, O, N, E = 512, 2048, 256, 512, 512, 128, 128, 256, 512


def setup_inputs():
    n = np.random.standard_normal
    idx = np.random.permutation(T)[:J]
    idx2 = np.random.permutation(T)[:J]
    idx3 = np.random.permutation(J)[:I]
    idx4 = np.stack([np.random.permutation(C)[:I] for _ in range(8)])
    idx5 = np.random.permutation(C)[:O]
    idx6 = np.random.permutation(J)[:O]
    idx7 = np.stack([np.random.permutation(E)[:O] for _ in range(8)])
    fk = mx_kscale(K)
    fr = mx_kscale(R)
    xtp = pack_weight(n((K, T)) / fk[:, None], "e2m1")
    wp = pack_weight(n((K, R)) * 1 / np.sqrt(K) * fk[:, None] * fr, "e4m3")
    w2p = pack_weight(n((K, R)) * 1 / np.sqrt(K) * fk[:, None] * fr, "e5m2")
    wbp = pack_weight(n((R, N)) * 1 / np.sqrt(R) / fr[:, None], "e2m1")
    return {
        "xt_words": xtp[0],
        "xt_scales": xtp[1],
        "w_words": wp[0],
        "w_scales": wp[1],
        "w2_words": w2p[0],
        "w2_scales": w2p[1],
        "sa": (np.random.uniform(0.5, 1.6, (R, 1))).astype(np.float32),
        "sb": (np.random.uniform(0.5, 1.6, (R, 1))).astype(np.float32),
        "wb_words": wbp[0],
        "wb_scales": wbp[1],
        "offs": striped(idx),
        "offs2": striped(idx2),
        "offs3": striped(idx3),
        "offs4": striped8(idx4),
        "offs5": striped(idx5),
        "offs6": striped(idx6),
        "offs7": striped8(idx7),
    }


def reference(xt_words, xt_scales, w_words, w_scales, w2_words, w2_scales, sa, sb, wb_words, wb_scales, offs, offs2, offs3, offs4, offs5, offs6, offs7):
    idx = unstriped(offs)
    idx2 = unstriped(offs2)
    idx3 = unstriped(offs3)
    idx4 = unstriped8(offs4)
    idx5 = unstriped(offs5)
    idx6 = unstriped(offs6)
    idx7 = unstriped8(offs7)
    xtu = unpack_weight(xt_words, xt_scales, "e2m1")
    wu = unpack_weight(w_words, w_scales, "e4m3")
    w2u = unpack_weight(w2_words, w2_scales, "e5m2")
    wbu = unpack_weight(wb_words, wb_scales, "e2m1")
    xtidxg = xtu[:, idx]
    a = wu.T @ xtidxg
    xtidx2g = xtu[:, idx2]
    b = w2u.T @ xtidx2g
    h1 = a[:, idx3] * f64(sa)
    pw = np.zeros((R, C))
    pw[np.arange(R)[:, None], idx4[np.arange(R) % 512 // 64]] = h1
    hid = np.abs(pw[:, idx5] - b[:, idx6] * f64(sb))
    hidq = mxq(hid, 0, "e5m2")
    p = wbu.T @ hidq
    y = np.zeros((N, E))
    y[np.arange(N)[:, None], idx7[np.arange(N) % 128 // 16]] = p
    return y

@@ -1,0 +1,189 @@
+from contextlib import ExitStack
+
+import concourse.mybir as mybir
+
+K, T, J, R, C, SEATS, PLACES, N, E = 512, 2048, 256, 512, 512, 128, 128, 256, 512
+FLOPS = 2 * K * R * J * 2 + 2 * R * N * PLACES
+
+F32 = mybir.dt.float32
+BF16 = mybir.dt.bfloat16
+I32 = mybir.dt.int32
+U32 = mybir.dt.uint32
+U16 = mybir.dt.uint16
+U8 = mybir.dt.uint8
+E4M3 = mybir.dt.float8_e4m3fn_x4
+E5M2 = mybir.dt.float8_e5m2_x4
+E2M1 = mybir.dt.float4_e2m1fn_x4
+COPY = mybir.ActivationFunctionType.Copy
+ABS = mybir.ActivationFunctionType.Abs
+ALU = mybir.AluOpType
+
+P = 128
+PACK = 4
+QUADS = 4
+
+
+def tile_list_ownseats_ahead_one_ownpage_kernel(
+    tc, xt_words, xt_scales, w_words, w_scales, w2_words, w2_scales, sa, sb, wb_words, wb_scales,
+    offs, offs2, offs3, offs4, offs5, offs6, offs7, out,
+):
+    nc = tc.nc
+    with ExitStack() as ctx:
+        sb_pool = ctx.enter_context(tc.tile_pool(name="sbuf", bufs=1))
+        psum = ctx.enter_context(tc.psum_pool(name="psum", bufs=1))
+
+        def sbuf(name, shape, dtype, tag=None):
+            return sb_pool.tile(shape, dtype, name=name, tag=tag or name, align_bytes=64)
+
+        def load_list(name, src):
+            lst = sb_pool.tile(list(src.shape), U16, name=name)
+            nc.sync.dma_start(lst[:], src)
+            return lst
+
+        def zeroed(name, shape, dtype):
+            t = sbuf(name, shape, dtype)
+            if dtype == U8:
+                nc.vector.memset(t[:].bitcast(I32), 0)
+            else:
+                nc.vector.memset(t[:], 0.0)
+            return t
+
+        def load_scale_rows(queue, plane, src):
+            for q in range(QUADS):
+                queue.dma_start(plane[32 * q : 32 * q + 4, :].bitcast(I32), src[0, 4 * q : 4 * q + 4, :].bitcast(I32))
+
+        def load_fp8_words(name, src):
+            t = sbuf(name, [P, R], U32)
+            nc.sync.dma_start(t[:].bitcast(I32), src[0].rearrange("p n t -> p (n t)").bitcast(I32))
+            return t
+
+        xs = zeroed("xs", [P, T], U8)
+        ws = zeroed("ws", [P, R], U8)
+        w2s = zeroed("w2s", [P, R], U8)
+        wbs = zeroed("wbs", [P, N], U8)
+
+        l1 = load_list("l1", offs)
+        xw = sbuf("xw", [P, T], U16)
+        nc.sync.dma_start(xw[:].bitcast(I32), xt_words[0].bitcast(I32))
+        load_scale_rows(nc.scalar, xs, xt_scales)
+        ws_stage = sbuf("ws_stage", [4, QUADS, R], U8)
+        nc.sync.dma_start(ws_stage[:].bitcast(I32), w_scales[0].rearrange("(q r) n -> r q n", r=4).bitcast(I32))
+        ww = load_fp8_words("ww", w_words)
+        sa_t = sbuf("sa_t", [P, PACK], F32)
+        nc.gpsimd.dma_start(sa_t[:], sa.rearrange("(p t) o -> p (t o)", t=PACK))
+        sb_t = sbuf("sb_t", [P, PACK], F32)
+        nc.gpsimd.dma_start(sb_t[:], sb.rearrange("(p t) o -> p (t o)", t=PACK))
+        l3 = load_list("l3", offs3)
+        l2 = load_list("l2", offs2)
+        l4 = load_list("l4", offs4)
+        w2w = load_fp8_words("w2w", w2_words)
+        load_scale_rows(nc.sync, w2s, w2_scales)
+        l6 = load_list("l6", offs6)
+        l5 = load_list("l5", offs5)
+        wbw = sbuf("wbw", [P, 2 * N], U8)
+        nc.sync.dma_start(wbw[:].bitcast(I32), wb_words[0].bitcast(I32))
+        load_scale_rows(nc.sync, wbs, wb_scales)
+        l7 = load_list("l7", offs7)
+
+        boards = [zeroed("board%d" % t, [P, C], F32) for t in range(PACK)]
+        pages = [zeroed("page%d" % m, [P, E], F32) for m in range(N // P)]
+
+        def gather(name, window, lst, dtype):
+            g = sbuf(name, [P, J], dtype)
+            nc.vector.tensor_copy(g[:], window[:].indirect(lst[:]))
+            return g
+
+        def dealt(tile_):
+            return tile_[:].rearrange("p t m -> p m t")
+
+        def by_t(tile_):
+            return tile_[:].rearrange("p (m t) -> p m t", t=PACK)
+
+        def product(bank, words, scales, fmt, gw, gs):
+            acc = psum.tile([P, J], F32, name=bank)
+            nc.tensor.matmul_mx(out=acc[:], lhsT=words.bitcast(fmt), lhsT_scale=scales,
+                                rhs=gw[:].bitcast(E2M1), rhs_scale=gs[:], start=True, stop=True)
+            return acc
+
+        def rows_to_sbuf(name, acc):
+            rows = sbuf(name, [P, J], F32)
+            nc.vector.tensor_copy(rows[:], acc[:])
+            return rows
+
+        g1s = gather("g1s", xs, l1, U8)
+        for q in range(QUADS):
+            nc.vector.tensor_copy(ws[32 * q : 32 * q + 4, :].bitcast(I32), ws_stage[:, q, :].bitcast(I32))
+        ws_d = sbuf("ws_d", [P, PACK, P], U8)
+        nc.vector.tensor_copy(dealt(ws_d), by_t(ws))
+        g1w = gather("g1w", xw, l1, U16)
+        w_first = sbuf("w_first", [P, P], U32)
+        nc.scalar.copy(w_first[:], by_t(ww)[:, :, 0])
+        w_rest = sbuf("w_rest", [P, PACK - 1, P], U32)
+        nc.scalar.copy(dealt(w_rest), by_t(ww)[:, :, 1:PACK])
+        w_of = [w_first[:]] + [w_rest[:, t, :] for t in range(PACK - 1)]
+        a_ps = [product("bank_a%d" % t, w_of[t], ws_d[:, t, :], E4M3, g1w, g1s) for t in range(PACK)]
+
+        a_rows = [rows_to_sbuf("a%d" % t, a_ps[t]) for t in range(PACK)]
+
+        def seat(t, tag=None):
+            h1 = sbuf("h1_%d" % t, [P, SEATS], F32, tag)
+            nc.scalar.activation(out=h1[:], in_=a_rows[t][:].indirect(l3[:]), func=COPY, scale=sa_t[:, t : t + 1])
+            return h1
+
+        def put(t, h1):
+            nc.scalar.activation(out=boards[t][:].indirect(l4[:]), in_=h1[:], func=COPY)
+
+        h1s = [seat(0), seat(1)]
+        put(0, h1s[0])
+        h1s.append(seat(2))
+        put(1, h1s[1])
+        put(2, h1s[2])
+
+        g2s = gather("g2s", xs, l2, U8)
+        g2w = gather("g2w", xw, l2, U16)
+        w2_d = sbuf("w2_d", [P, PACK, P], U32)
+        nc.vector.tensor_copy(dealt(w2_d), by_t(w2w))
+        w2s_d = sbuf("w2s_d", [P, PACK, P], U8)
+        nc.vector.tensor_copy(dealt(w2s_d), by_t(w2s))
+        b_ps = [product("bank_b%d" % t, w2_d[:, t, :], w2s_d[:, t, :], E5M2, g2w, g2s) for t in range(PACK)]
+        b_rows = [rows_to_sbuf("b%d" % t, b_ps[t]) for t in range(PACK)]
+
+        diff = [sbuf("diff%d" % u, [P, 2, PLACES], F32) for u in range(2)]
+        hid = sbuf("hid", [P, PLACES, PACK], BF16)
+        picked = []
+        for t in range(PACK):
+            pb = sbuf("pb%d" % t, [P, PLACES], F32)
+            nc.scalar.activation(out=pb[:], in_=b_rows[t][:].indirect(l6[:]), func=COPY, scale=sb_t[:, t : t + 1])
+            picked.append(pb)
+            if t == 2:
+                h1s.append(seat(3, "b2"))
+        put(3, h1s[3])
+
+        def difference(t):
+            nc.vector.tensor_tensor(diff[t // 2][:, t % 2, :], boards[t][:].indirect(l5[:]), picked[t][:], ALU.subtract)
+
+        def magnitude(u):
+            d = diff[u][:].rearrange("p t o -> p o t")
+            nc.vector.scalar_tensor_tensor(out=hid[:, :, 2 * u : 2 * u + 2], in0=d, scalar=-1.0, in1=d,
+                                           op0=ALU.mult, op1=ALU.max)
+
+        difference(0)
+        difference(1)
+        difference(2)
+        magnitude(0)
+        difference(3)
+        nc.scalar.activation(out=hid[:, :, 2:4], in_=diff[1][:].rearrange("p t o -> p o t"), func=ABS)
+
+        hq = sbuf("hq", [P, PLACES], U32)
+        hs = sbuf("hs", [P, PLACES], U8)
+        nc.vector.quantize_mx(out=hq[:].bitcast(E5M2), scales=hs[:], in_=hid[:].rearrange("p o t -> p (o t)"))
+
+        for m in range(N // P):
+            acc = psum.tile([P, PLACES], F32, name="bank_a%d" % m)
+            nc.tensor.matmul_mx(out=acc[:], lhsT=wbw[:, 2 * P * m : 2 * P * (m + 1)].bitcast(E2M1),
+                                lhsT_scale=wbs[:, P * m : P * (m + 1)], rhs=hq[:].bitcast(E5M2), rhs_scale=hs[:],
+                                start=True, stop=True)
+            res = sbuf("res%d" % m, [P, PLACES], F32)
+            nc.vector.tensor_copy(res[:], acc[:])
+            nc.scalar.activation(out=pages[m][:].indirect(l7[:]), in_=res[:], func=COPY)
+            nc.sync.dma_start(out[P * m : P * (m + 1), :], pages[m][:])

@@ -42,10 +42,7 @@ def tile_list_ownseats_ahead_one_ownpage_kernel(
 
         def zeroed(name, shape, dtype):
             t = sbuf(name, shape, dtype)
-            if dtype == U8:
-                nc.vector.memset(t[:].bitcast(I32), 0)
-            else:
-                nc.vector.memset(t[:], 0.0)
+            nc.vector.memset(t[:].bitcast(I32), 0)
             return t
 
         def load_scale_rows(queue, plane, src):
@@ -53,7 +50,7 @@ def tile_list_ownseats_ahead_one_ownpage_kernel(
                 queue.dma_start(plane[32 * q : 32 * q + 4, :].bitcast(I32), src[0, 4 * q : 4 * q + 4, :].bitcast(I32))
 
         def load_fp8_words(name, src):
-            t = sbuf(name, [P, R], U32)
+            t = sbuf(name, [P, R], U32, name)
             nc.sync.dma_start(t[:].bitcast(I32), src[0].rearrange("p n t -> p (n t)").bitcast(I32))
             return t
 
@@ -63,11 +60,11 @@ def tile_list_ownseats_ahead_one_ownpage_kernel(
         wbs = zeroed("wbs", [P, N], U8)
 
         l1 = load_list("l1", offs)
+        ws_stage = sbuf("ws_stage", [4, QUADS, R], U8)
+        nc.sync.dma_start(ws_stage[:].bitcast(I32), w_scales[0].rearrange("(q r) n -> r q n", r=4).bitcast(I32))
         xw = sbuf("xw", [P, T], U16)
         nc.sync.dma_start(xw[:].bitcast(I32), xt_words[0].bitcast(I32))
         load_scale_rows(nc.scalar, xs, xt_scales)
-        ws_stage = sbuf("ws_stage", [4, QUADS, R], U8)
-        nc.sync.dma_start(ws_stage[:].bitcast(I32), w_scales[0].rearrange("(q r) n -> r q n", r=4).bitcast(I32))
         ww = load_fp8_words("ww", w_words)
         sa_t = sbuf("sa_t", [P, PACK], F32)
         nc.gpsimd.dma_start(sa_t[:], sa.rearrange("(p t) o -> p (t o)", t=PACK))
@@ -88,8 +85,8 @@ def tile_list_ownseats_ahead_one_ownpage_kernel(
         boards = [zeroed("board%d" % t, [P, C], F32) for t in range(PACK)]
         pages = [zeroed("page%d" % m, [P, E], F32) for m in range(N // P)]
 
-        def gather(name, window, lst, dtype):
-            g = sbuf(name, [P, J], dtype)
+        def gather(name, window, lst, dtype, tag=None):
+            g = sbuf(name, [P, J], dtype, tag)
             nc.vector.tensor_copy(g[:], window[:].indirect(lst[:]))
             return g
 
@@ -105,25 +102,33 @@ def tile_list_ownseats_ahead_one_ownpage_kernel(
                                 rhs=gw[:].bitcast(E2M1), rhs_scale=gs[:], start=True, stop=True)
             return acc
 
-        def rows_to_sbuf(name, acc):
-            rows = sbuf(name, [P, J], F32)
-            nc.vector.tensor_copy(rows[:], acc[:])
+        def rows_to_sbuf(name, acc, tag=None):
+            rows = sbuf(name, [P, J], F32, tag)
+            if name == "a0":
+                nc.scalar.copy(rows[:], acc[:])
+            else:
+                nc.vector.tensor_copy(rows[:], acc[:])
             return rows
 
-        g1s = gather("g1s", xs, l1, U8)
         for q in range(QUADS):
             nc.vector.tensor_copy(ws[32 * q : 32 * q + 4, :].bitcast(I32), ws_stage[:, q, :].bitcast(I32))
-        ws_d = sbuf("ws_d", [P, PACK, P], U8)
-        nc.vector.tensor_copy(dealt(ws_d), by_t(ws))
+        ws_by_t = ws[:].rearrange("p (m t) -> p t m", t=PACK)
+        ws_first = sbuf("ws_first", [P, P], U8)
+        nc.vector.tensor_copy(ws_first[:], ws_by_t[:, 0, :])
+        g1s = gather("g1s", xs, l1, U8)
         g1w = gather("g1w", xw, l1, U16)
+        ws_rest = sbuf("ws_rest", [P, PACK - 1, P], U8)
+        nc.vector.tensor_copy(ws_rest[:], ws_by_t[:, 1:PACK, :])
+        ws_of = [ws_first[:]] + [ws_rest[:, t, :] for t in range(PACK - 1)]
+        g2w = gather("g2w", xw, l2, U16)
         w_first = sbuf("w_first", [P, P], U32)
         nc.scalar.copy(w_first[:], by_t(ww)[:, :, 0])
         w_rest = sbuf("w_rest", [P, PACK - 1, P], U32)
         nc.scalar.copy(dealt(w_rest), by_t(ww)[:, :, 1:PACK])
         w_of = [w_first[:]] + [w_rest[:, t, :] for t in range(PACK - 1)]
-        a_ps = [product("bank_a%d" % t, w_of[t], ws_d[:, t, :], E4M3, g1w, g1s) for t in range(PACK)]
+        a_ps = [product("bank_a%d" % t, w_of[t], ws_of[t], E4M3, g1w, g1s) for t in range(PACK)]
 
-        a_rows = [rows_to_sbuf("a%d" % t, a_ps[t]) for t in range(PACK)]
+        a_rows = [rows_to_sbuf("a%d" % t, a_ps[t]) for t in range(PACK - 1)]
 
         def seat(t, tag=None):
             h1 = sbuf("h1_%d" % t, [P, SEATS], F32, tag)
@@ -139,16 +144,18 @@ def tile_list_ownseats_ahead_one_ownpage_kernel(
         put(1, h1s[1])
         put(2, h1s[2])
 
-        g2s = gather("g2s", xs, l2, U8)
-        g2w = gather("g2w", xw, l2, U16)
-        w2_d = sbuf("w2_d", [P, PACK, P], U32)
-        nc.vector.tensor_copy(dealt(w2_d), by_t(w2w))
-        w2s_d = sbuf("w2s_d", [P, PACK, P], U8)
-        nc.vector.tensor_copy(dealt(w2s_d), by_t(w2s))
+        g2s = gather("g2s", xs, l2, U8, "g1s")
+        w2_d = sbuf("w2_d", [P, PACK, P], U32, "w_rest")
+        nc.vector.tensor_copy(w2_d[:].rearrange("p t (c i) -> p c t i", i=4),
+                              w2w[:].rearrange("p (c i t) -> p c t i", i=4, t=PACK))
+        w2s_d = sbuf("w2s_d", [P, PACK, P], U8, "ws_rest")
+        nc.vector.tensor_copy(w2s_d[:], w2s[:].rearrange("p (m t) -> p t m", t=PACK))
         b_ps = [product("bank_b%d" % t, w2_d[:, t, :], w2s_d[:, t, :], E5M2, g2w, g2s) for t in range(PACK)]
-        b_rows = [rows_to_sbuf("b%d" % t, b_ps[t]) for t in range(PACK)]
+        b_rows = [rows_to_sbuf("b%d" % t, b_ps[t]) for t in range(PACK - 1)]
+        a_rows.append(rows_to_sbuf("a3", a_ps[3], "a0"))
+        b_rows.append(rows_to_sbuf("b3", b_ps[3]))
 
-        diff = [sbuf("diff%d" % u, [P, 2, PLACES], F32) for u in range(2)]
+        diff = sbuf("diff", [P, PACK, PLACES], F32)
         hid = sbuf("hid", [P, PLACES, PACK], BF16)
         picked = []
         for t in range(PACK):
@@ -160,19 +167,12 @@ def tile_list_ownseats_ahead_one_ownpage_kernel(
         put(3, h1s[3])
 
         def difference(t):
-            nc.vector.tensor_tensor(diff[t // 2][:, t % 2, :], boards[t][:].indirect(l5[:]), picked[t][:], ALU.subtract)
+            nc.vector.tensor_tensor(diff[:, t, :], boards[t][:].indirect(l5[:]), picked[t][:], ALU.subtract)
 
-        def magnitude(u):
-            d = diff[u][:].rearrange("p t o -> p o t")
-            nc.vector.scalar_tensor_tensor(out=hid[:, :, 2 * u : 2 * u + 2], in0=d, scalar=-1.0, in1=d,
-                                           op0=ALU.mult, op1=ALU.max)
-
-        difference(0)
-        difference(1)
-        difference(2)
-        magnitude(0)
-        difference(3)
-        nc.scalar.activation(out=hid[:, :, 2:4], in_=diff[1][:].rearrange("p t o -> p o t"), func=ABS)
+        for t in range(PACK):
+            difference(t)
+        nc.scalar.activation(out=hid[:].rearrange("p (c i) t -> p c t i", i=4),
+                             in_=diff[:].rearrange("p t (c i) -> p c t i", i=4), func=ABS)
 
         hq = sbuf("hq", [P, PLACES], U32)
         hs = sbuf("hs", [P, PLACES], U8)

from contextlib import ExitStack

import concourse.mybir as mybir

K, T, J, R, C, SEATS, PLACES, N, E = 512, 2048, 256, 512, 512, 128, 128, 256, 512
FLOPS = 2 * K * R * J * 2 + 2 * R * N * PLACES

F32 = mybir.dt.float32
BF16 = mybir.dt.bfloat16
I32 = mybir.dt.int32
U32 = mybir.dt.uint32
U16 = mybir.dt.uint16
U8 = mybir.dt.uint8
E4M3 = mybir.dt.float8_e4m3fn_x4
E5M2 = mybir.dt.float8_e5m2_x4
E2M1 = mybir.dt.float4_e2m1fn_x4
COPY = mybir.ActivationFunctionType.Copy
ABS = mybir.ActivationFunctionType.Abs
ALU = mybir.AluOpType

P = 128
PACK = 4
QUADS = 4


def tile_list_ownseats_ahead_one_ownpage_kernel(
    tc, xt_words, xt_scales, w_words, w_scales, w2_words, w2_scales, sa, sb, wb_words, wb_scales,
    offs, offs2, offs3, offs4, offs5, offs6, offs7, out,
):
    nc = tc.nc
    with ExitStack() as ctx:
        sb_pool = ctx.enter_context(tc.tile_pool(name="sbuf", bufs=1))
        psum = ctx.enter_context(tc.psum_pool(name="psum", bufs=1))

        def sbuf(name, shape, dtype, tag=None):
            return sb_pool.tile(shape, dtype, name=name, tag=tag or name, align_bytes=64)

        def load_list(name, src):
            lst = sb_pool.tile(list(src.shape), U16, name=name)
            nc.sync.dma_start(lst[:], src)
            return lst

        def zeroed(name, shape, dtype):
            t = sbuf(name, shape, dtype)
            nc.vector.memset(t[:].bitcast(I32), 0)
            return t

        def load_scale_rows(queue, plane, src):
            for q in range(QUADS):
                queue.dma_start(plane[32 * q : 32 * q + 4, :].bitcast(I32), src[0, 4 * q : 4 * q + 4, :].bitcast(I32))

        def load_fp8_words(name, src):
            t = sbuf(name, [P, R], U32, name)
            nc.sync.dma_start(t[:].bitcast(I32), src[0].rearrange("p n t -> p (n t)").bitcast(I32))
            return t

        xs = zeroed("xs", [P, T], U8)
        ws = zeroed("ws", [P, R], U8)
        w2s = zeroed("w2s", [P, R], U8)
        wbs = zeroed("wbs", [P, N], U8)

        l1 = load_list("l1", offs)
        ws_stage = sbuf("ws_stage", [4, QUADS, R], U8)
        nc.sync.dma_start(ws_stage[:].bitcast(I32), w_scales[0].rearrange("(q r) n -> r q n", r=4).bitcast(I32))
        xw = sbuf("xw", [P, T], U16)
        nc.sync.dma_start(xw[:].bitcast(I32), xt_words[0].bitcast(I32))
        load_scale_rows(nc.scalar, xs, xt_scales)
        ww = load_fp8_words("ww", w_words)
        sa_t = sbuf("sa_t", [P, PACK], F32)
        nc.gpsimd.dma_start(sa_t[:], sa.rearrange("(p t) o -> p (t o)", t=PACK))
        sb_t = sbuf("sb_t", [P, PACK], F32)
        nc.gpsimd.dma_start(sb_t[:], sb.rearrange("(p t) o -> p (t o)", t=PACK))
        l3 = load_list("l3", offs3)
        l2 = load_list("l2", offs2)
        l4 = load_list("l4", offs4)
        w2w = load_fp8_words("w2w", w2_words)
        load_scale_rows(nc.sync, w2s, w2_scales)
        l6 = load_list("l6", offs6)
        l5 = load_list("l5", offs5)
        wbw = sbuf("wbw", [P, 2 * N], U8)
        nc.sync.dma_start(wbw[:].bitcast(I32), wb_words[0].bitcast(I32))
        load_scale_rows(nc.sync, wbs, wb_scales)
        l7 = load_list("l7", offs7)

        boards = [zeroed("board%d" % t, [P, C], F32) for t in range(PACK)]
        pages = [zeroed("page%d" % m, [P, E], F32) for m in range(N // P)]

        def gather(name, window, lst, dtype, tag=None):
            g = sbuf(name, [P, J], dtype, tag)
            nc.vector.tensor_copy(g[:], window[:].indirect(lst[:]))
            return g

        def dealt(tile_):
            return tile_[:].rearrange("p t m -> p m t")

        def by_t(tile_):
            return tile_[:].rearrange("p (m t) -> p m t", t=PACK)

        def product(bank, words, scales, fmt, gw, gs):
            acc = psum.tile([P, J], F32, name=bank)
            nc.tensor.matmul_mx(out=acc[:], lhsT=words.bitcast(fmt), lhsT_scale=scales,
                                rhs=gw[:].bitcast(E2M1), rhs_scale=gs[:], start=True, stop=True)
            return acc

        def rows_to_sbuf(name, acc, tag=None):
            rows = sbuf(name, [P, J], F32, tag)
            if name == "a0":
                nc.scalar.copy(rows[:], acc[:])
            else:
                nc.vector.tensor_copy(rows[:], acc[:])
            return rows

        for q in range(QUADS):
            nc.vector.tensor_copy(ws[32 * q : 32 * q + 4, :].bitcast(I32), ws_stage[:, q, :].bitcast(I32))
        ws_by_t = ws[:].rearrange("p (m t) -> p t m", t=PACK)
        ws_first = sbuf("ws_first", [P, P], U8)
        nc.vector.tensor_copy(ws_first[:], ws_by_t[:, 0, :])
        g1s = gather("g1s", xs, l1, U8)
        g1w = gather("g1w", xw, l1, U16)
        ws_rest = sbuf("ws_rest", [P, PACK - 1, P], U8)
        nc.vector.tensor_copy(ws_rest[:], ws_by_t[:, 1:PACK, :])
        ws_of = [ws_first[:]] + [ws_rest[:, t, :] for t in range(PACK - 1)]
        g2w = gather("g2w", xw, l2, U16)
        w_first = sbuf("w_first", [P, P], U32)
        nc.scalar.copy(w_first[:], by_t(ww)[:, :, 0])
        w_rest = sbuf("w_rest", [P, PACK - 1, P], U32)
        nc.scalar.copy(dealt(w_rest), by_t(ww)[:, :, 1:PACK])
        w_of = [w_first[:]] + [w_rest[:, t, :] for t in range(PACK - 1)]
        a_ps = [product("bank_a%d" % t, w_of[t], ws_of[t], E4M3, g1w, g1s) for t in range(PACK)]

        a_rows = [rows_to_sbuf("a%d" % t, a_ps[t]) for t in range(PACK - 1)]

        def seat(t, tag=None):
            h1 = sbuf("h1_%d" % t, [P, SEATS], F32, tag)
            nc.scalar.activation(out=h1[:], in_=a_rows[t][:].indirect(l3[:]), func=COPY, scale=sa_t[:, t : t + 1])
            return h1

        def put(t, h1):
            nc.scalar.activation(out=boards[t][:].indirect(l4[:]), in_=h1[:], func=COPY)

        h1s = [seat(0), seat(1)]
        put(0, h1s[0])
        h1s.append(seat(2))
        put(1, h1s[1])
        put(2, h1s[2])

        g2s = gather("g2s", xs, l2, U8, "g1s")
        w2_d = sbuf("w2_d", [P, PACK, P], U32, "w_rest")
        nc.vector.tensor_copy(w2_d[:].rearrange("p t (c i) -> p c t i", i=4),
                              w2w[:].rearrange("p (c i t) -> p c t i", i=4, t=PACK))
        w2s_d = sbuf("w2s_d", [P, PACK, P], U8, "ws_rest")
        nc.vector.tensor_copy(w2s_d[:], w2s[:].rearrange("p (m t) -> p t m", t=PACK))
        b_ps = [product("bank_b%d" % t, w2_d[:, t, :], w2s_d[:, t, :], E5M2, g2w, g2s) for t in range(PACK)]
        b_rows = [rows_to_sbuf("b%d" % t, b_ps[t]) for t in range(PACK - 1)]
        a_rows.append(rows_to_sbuf("a3", a_ps[3], "a0"))
        b_rows.append(rows_to_sbuf("b3", b_ps[3]))

        diff = sbuf("diff", [P, PACK, PLACES], F32)
        hid = sbuf("hid", [P, PLACES, PACK], BF16)
        picked = []
        for t in range(PACK):
            pb = sbuf("pb%d" % t, [P, PLACES], F32)
            nc.scalar.activation(out=pb[:], in_=b_rows[t][:].indirect(l6[:]), func=COPY, scale=sb_t[:, t : t + 1])
            picked.append(pb)
            if t == 2:
                h1s.append(seat(3, "b2"))
        put(3, h1s[3])

        def difference(t):
            nc.vector.tensor_tensor(diff[:, t, :], boards[t][:].indirect(l5[:]), picked[t][:], ALU.subtract)

        for t in range(PACK):
            difference(t)
        nc.scalar.activation(out=hid[:].rearrange("p (c i) t -> p c t i", i=4),
                             in_=diff[:].rearrange("p t (c i) -> p c t i", i=4), func=ABS)

        hq = sbuf("hq", [P, PLACES], U32)
        hs = sbuf("hs", [P, PLACES], U8)
        nc.vector.quantize_mx(out=hq[:].bitcast(E5M2), scales=hs[:], in_=hid[:].rearrange("p o t -> p (o t)"))

        for m in range(N // P):
            acc = psum.tile([P, PLACES], F32, name="bank_a%d" % m)
            nc.tensor.matmul_mx(out=acc[:], lhsT=wbw[:, 2 * P * m : 2 * P * (m + 1)].bitcast(E2M1),
                                lhsT_scale=wbs[:, P * m : P * (m + 1)], rhs=hq[:].bitcast(E5M2), rhs_scale=hs[:],
                                start=True, stop=True)
            res = sbuf("res%d" % m, [P, PLACES], F32)
            nc.vector.tensor_copy(res[:], acc[:])
            nc.scalar.activation(out=pages[m][:].indirect(l7[:]), in_=res[:], func=COPY)
            nc.sync.dma_start(out[P * m : P * (m + 1), :], pages[m][:])
